import numpy as np
import ml_dtypes


def mxq(x, axis, fmt="e4m3"):
    dtype, down = {"e4m3": (ml_dtypes.float8_e4m3fn, 7), "e5m2": (ml_dtypes.float8_e5m2, 14)}[fmt]
    v = np.moveaxis(np.asarray(x, np.float32).astype(ml_dtypes.bfloat16).astype(np.float64), axis, -1)
    blocks = v.reshape(v.shape[:-1] + (-1, 32))
    amax = np.abs(blocks).max(-1, keepdims=True)
    byte = np.maximum(np.where(amax > 0, np.frexp(amax)[1] - 1 + 127, 0) - down, 1)
    scale = np.exp2(byte - 127.0)
    codes = (blocks / scale).astype(np.float32).astype(dtype).astype(np.float64)
    return np.moveaxis((codes * scale).reshape(v.shape), -1, axis)


WIDE = False


def mx_kscale(k):
    if not WIDE:
        return np.ones(k)
    levels = np.array([10, -10, 5, -5, 0])
    if k % 512:
        return np.exp2(np.random.permutation(np.resize(levels, k // 32))).repeat(32)
    a = np.empty((k // 512, 16))
    for p in range(k // 512):
        a[p, :8] = np.random.permutation(np.resize(levels, 8))
        for g in range(8):
            far = levels[np.abs(levels - a[p, g]) >= 10]
            a[p, g + 8] = far[np.random.randint(len(far))]
    return np.exp2(a.ravel()).repeat(32)


def f64(x):
    return np.asarray(x).astype(np.float64)


def striped8(idx):
    return np.asarray(idx).reshape(8, -1, 16).transpose(0, 2, 1).reshape(128, -1).astype(np.uint16)


def unstriped8(offs):
    return offs.reshape(8, 16, -1).transpose(0, 2, 1).reshape(8, -1).astype(np.int64)


def pick8(x, idx, run):
    r = np.arange(len(x))
    return x[r[:, None], idx[r % (8 * run) // run]]


E2M1 = np.array([0.0, 0.5, 1.0, 1.5, 2.0, 3.0, 4.0, 6.0, -0.0, -0.5, -1.0, -1.5, -2.0, -3.0, -4.0, -6.0])


def pack_weight(w, fmt):
    k, n = w.shape
    w = f64(np.asarray(w, np.float32).astype(ml_dtypes.bfloat16)).reshape(k // 32, 32, n)
    amax = np.abs(w).max(1)
    if fmt == "e4m3":
        byte = np.frexp(amax)[1] - 1 + 127 - 7
    else:
        mant, ex = np.frexp(amax / 6.0)
        byte = np.where(mant > 0.5, ex, ex - 1) + 127
    byte = np.clip(np.where(amax > 0, byte, 1), 1, 254)
    scaled = (w * np.exp2(127.0 - byte)[:, None, :]).reshape(k, n).astype(np.float32)
    by_word = np.ascontiguousarray(scaled.reshape(k // 512, 128, 4, n).transpose(0, 1, 3, 2))
    if fmt == "e4m3":
        words = by_word.astype(ml_dtypes.float8_e4m3fn).view(np.uint8)
    else:
        c = by_word.astype(ml_dtypes.float4_e2m1fn).view(np.uint8) & 0xF
        words = (c[..., 0::2] | (c[..., 1::2] << 4)).reshape(k // 512, 128, 2 * n)
    return np.ascontiguousarray(words), np.ascontiguousarray(byte.astype(np.uint8).reshape(k // 512, 16, n))


def unpack_weight(words, scales, fmt):
    g, _, n = scales.shape
    words = np.ascontiguousarray(words).reshape(g, 128, n, -1)
    if fmt == "e4m3":
        vals = words.view(ml_dtypes.float8_e4m3fn).astype(np.float64)
    else:
        nib = np.empty((g, 128, n, 4), np.uint8)
        nib[..., 0::2] = words & 0xF
        nib[..., 1::2] = words >> 4
        vals = E2M1[nib]
    vals = vals * np.repeat(np.exp2(scales.astype(np.float64) - 127.0), 8, axis=1)[..., None]
    return vals.transpose(0, 1, 3, 2).reshape(g * 512, n)


D, T, I, Q = 512, 1024, 512, 128


def setup_inputs():
    n = np.random.standard_normal
    idx = np.stack([np.random.permutation(T)[:I] for _ in range(8)])
    idx2 = np.stack([np.random.permutation(T)[:I] for _ in range(8)])
    fd = mx_kscale(D)
    keysp = pack_weight(n((D, T)) / fd[:, None], "e4m3")
    return {
        "query": (n((D, Q)) * 0.9 / np.sqrt(D) * fd[:, None]).astype(np.float32),
        "query2": (n((D, Q)) * 0.9 / np.sqrt(D) * fd[:, None]).astype(np.float32),
        "keys_words": keysp[0],
        "keys_scales": keysp[1],
        "lam": (np.random.uniform(0.5, 1.5, (Q, 1))).astype(np.float32),
        "damp": (np.random.uniform(1.0, 4.0, (Q, 1))).astype(np.float32),
        "old": (np.random.uniform(0.0, 2.0, (Q, T))).astype(np.float32),
        "fade": (np.random.uniform(0.3, 0.9, (Q, 1))).astype(np.float32),
        "offs": striped8(idx),
        "offs2": striped8(idx2),
    }


def reference(query, query2, keys_words, keys_scales, lam, damp, old, fade, offs, offs2):
    idx = unstriped8(offs)
    idx2 = unstriped8(offs2)
    keysu = unpack_weight(keys_words, keys_scales, "e4m3")
    queryq = mxq(f64(query), 0, "e4m3")
    a = queryq.T @ keysu
    query2q = mxq(f64(query2), 0, "e4m3")
    b = query2q.T @ keysu
    s = pick8(a, idx, 16) + pick8(a, idx2, 16) * np.tanh(pick8(b, idx, 16)) * f64(lam)
    p = np.exp(s - np.max(s, axis=1, keepdims=True))
    r = p / np.sum(p, axis=1, keepdims=True) * 512.0
    u0 = np.log(r * f64(damp) + 1.0)
    w = u0 / np.sum(u0, axis=1, keepdims=True)
    ws = w * 512.0
    wf = np.zeros((Q, T))
    wf[np.arange(Q)[:, None], idx[np.arange(Q) % 128 // 16]] = ws
    y = f64(old) * f64(fade) + wf
    return y

@@ -1,0 +1,154 @@
+from contextlib import ExitStack
+
+import concourse.mybir as mybir
+
+D, T, I, Q = 512, 1024, 512, 128
+FLOPS = 2 * 2 * D * T * Q
+
+F32 = mybir.dt.float32
+BF16 = mybir.dt.bfloat16
+I32 = mybir.dt.int32
+U32 = mybir.dt.uint32
+U16 = mybir.dt.uint16
+U8 = mybir.dt.uint8
+FP8X4 = mybir.dt.float8_e4m3fn_x4
+ALU = mybir.AluOpType
+ACT = mybir.ActivationFunctionType
+
+P = 128
+PACK = 4
+HALF = T // 2
+STORE = 256
+
+
+def tile_attend_turnedby_dampened_counts_heads_kernel(
+    tc, query, query2, keys_words, keys_scales, lam, damp, old, fade, offs, offs2, out
+):
+    nc = tc.nc
+    with ExitStack() as ctx:
+        sb = ctx.enter_context(tc.tile_pool(name="sb", bufs=1))
+        ps = ctx.enter_context(tc.psum_pool(name="ps", bufs=1))
+
+        idx = sb.tile([P, I // 16], U16, name="idx")
+        idx2 = sb.tile([P, I // 16], U16, name="idx2")
+        raw_b = sb.tile([P, PACK, Q], F32, name="raw_b")
+        raw_a = sb.tile([P, PACK, Q], F32, name="raw_a")
+        words = [sb.tile([P, HALF], U32, name=f"words{h}", align_bytes=64) for h in range(2)]
+        planes = sb.tile([P, T], U8, name="planes", align_bytes=64)
+        lam_t = sb.tile([P, 1], F32, name="lam_t")
+        damp_t = sb.tile([P, 1], F32, name="damp_t")
+        fade_t = sb.tile([P, 1], F32, name="fade_t")
+        old_t = sb.tile([P, T], F32, name="old_t")
+
+        word_bytes = keys_words[0].rearrange("p n t -> p (n t)")
+
+        def load_words(h):
+            nc.sync.dma_start(
+                out=words[h][:].bitcast(I32),
+                in_=word_bytes[:, PACK * HALF * h : PACK * HALF * (h + 1)].bitcast(I32),
+            )
+
+        nc.sync.dma_start(out=raw_b[:], in_=query2.rearrange("(p j) w -> p j w", j=PACK))
+        for quad in range(4):
+            nc.scalar.dma_start(
+                out=planes[32 * quad : 32 * quad + 4, :].bitcast(I32),
+                in_=keys_scales[0, 4 * quad : 4 * quad + 4, :].bitcast(I32),
+            )
+        load_words(0)
+        nc.sync.dma_start(out=raw_a[:], in_=query.rearrange("(p j) w -> p j w", j=PACK))
+        load_words(1)
+        nc.sync.dma_start(idx[:], offs)
+        nc.sync.dma_start(idx2[:], offs2)
+        nc.sync.dma_start(out=old_t[:], in_=old)
+        nc.gpsimd.dma_start(out=lam_t[:], in_=lam)
+        nc.gpsimd.dma_start(out=damp_t[:], in_=damp)
+        nc.gpsimd.dma_start(out=fade_t[:], in_=fade)
+
+        wf = sb.tile([P, T], F32, name="wf")
+        nc.vector.memset(wf[:], 0.0)
+
+        def quantise(raw, name):
+            grouped = sb.tile([P, Q, PACK], BF16, name=name + "_bf", align_bytes=64)
+            codes = sb.tile([P, Q], U32, name=name + "_codes", align_bytes=64)
+            scales = sb.tile([P, Q], U8, name=name + "_scales", align_bytes=64)
+            nc.vector.tensor_copy(out=grouped[:], in_=raw[:].rearrange("p j w -> p w j"))
+            nc.vector.quantize_mx(
+                out=codes[:].bitcast(FP8X4), scales=scales[:], in_=grouped[:].rearrange("p w j -> p (w j)")
+            )
+            return codes, scales
+
+        def score(operand, h, name):
+            codes, scales = operand
+            bank = ps.tile([P, HALF], F32, name=name)
+            nc.tensor.matmul_mx(
+                out=bank[:],
+                lhsT=codes[:].bitcast(FP8X4),
+                lhsT_scale=scales[:],
+                rhs=words[h][:].bitcast(FP8X4),
+                rhs_scale=planes[:, HALF * h : HALF * (h + 1)],
+                start=True,
+                stop=True,
+            )
+            return bank
+
+        a_sb = sb.tile([P, T], F32, name="a_sb")
+        b_sb = sb.tile([P, T], F32, name="b_sb")
+
+        qb = quantise(raw_b, "qb")
+        b0 = score(qb, 0, "b0")
+        qa = quantise(raw_a, "qa")
+        nc.scalar.activation(out=b_sb[:, :HALF], in_=b0[:], func=ACT.Copy)
+        b1 = score(qb, 1, "b1")
+        nc.vector.tensor_copy(out=b_sb[:, HALF:], in_=b1[:])
+        a0 = score(qa, 0, "a0")
+        a1 = score(qa, 1, "a1")
+        nc.scalar.copy(out=a_sb[:, :HALF], in_=a0[:])
+        nc.scalar.copy(out=a_sb[:, HALF:], in_=a1[:])
+
+        b_at = sb.tile([P, I], F32, name="b_at")
+        turn = sb.tile([P, I], F32, name="turn")
+        a_at = sb.tile([P, I], F32, name="a_at")
+        a_at2 = sb.tile([P, I], F32, name="a_at2")
+        nc.vector.tensor_copy(out=b_at[:], in_=b_sb[:].indirect(idx[:]))
+        nc.scalar.activation(out=turn[:], in_=b_at[:], func=ACT.Tanh)
+        nc.vector.tensor_copy(out=a_at2[:], in_=a_sb[:].indirect(idx2[:]))
+        nc.scalar.activation(out=a_at[:], in_=a_sb[:].indirect(idx[:]), func=ACT.Copy)
+
+        term = sb.tile([P, I], F32, name="term")
+        s = sb.tile([P, I], F32, name="s")
+        neg_max = sb.tile([P, 1], F32, name="neg_max")
+        nc.vector.scalar_tensor_tensor(
+            out=term[:], in0=turn[:], scalar=lam_t[:], in1=a_at2[:], op0=ALU.mult, op1=ALU.mult
+        )
+        nc.vector.tensor_tensor(out=s[:], in0=term[:], in1=a_at[:], op=ALU.add)
+        nc.vector.tensor_reduce(out=neg_max[:], in_=s[:], axis=mybir.AxisListType.X, op=ALU.max, negate=True)
+
+        p = sb.tile([P, I], F32, name="p")
+        p_sum = sb.tile([P, 1], F32, name="p_sum")
+        p_inv = sb.tile([P, 1], F32, name="p_inv")
+        gain = sb.tile([P, 1], F32, name="gain")
+        nc.scalar.activation(out=p[:], in_=s[:], func=ACT.Exp, bias=neg_max[:], accum_out=p_sum[:])
+        nc.vector.reciprocal(out=p_inv[:], in_=p_sum[:])
+        nc.vector.tensor_scalar(
+            out=gain[:], in0=p_inv[:], scalar1=damp_t[:], scalar2=float(I), op0=ALU.mult, op1=ALU.mult
+        )
+
+        part = sb.tile([P, I], F32, name="part")
+        part_sum = sb.tile([P, 1], F32, name="part_sum")
+        part_inv = sb.tile([P, 1], F32, name="part_inv")
+        ws = sb.tile([P, I], F32, name="ws")
+        nc.scalar.activation(out=part[:], in_=p[:], func=ACT.Ln, scale=gain[:], bias=1.0, accum_out=part_sum[:])
+        nc.vector.reciprocal(out=part_inv[:], in_=part_sum[:])
+        nc.vector.tensor_scalar(
+            out=ws[:], in0=part[:], scalar1=part_inv[:], scalar2=float(I), op0=ALU.mult, op1=ALU.mult
+        )
+        nc.vector.tensor_copy(out=wf[:].indirect(idx[:]), in_=ws[:])
+
+        for c in range(T // STORE):
+            cols = slice(STORE * c, STORE * (c + 1))
+            y = sb.tile([P, STORE], F32, name=f"y{c}")
+            nc.vector.scalar_tensor_tensor(
+                out=y[:], in0=old_t[:, cols], scalar=fade_t[:], in1=wf[:, cols], op0=ALU.mult, op1=ALU.add
+            )
+            queue = nc.sync if c % 2 == 0 else nc.scalar
+            queue.dma_start(out=out[:, cols], in_=y[:])

@@ -33,7 +33,8 @@ def tile_attend_turnedby_dampened_counts_heads_kernel(
         idx2 = sb.tile([P, I // 16], U16, name="idx2")
         raw_b = sb.tile([P, PACK, Q], F32, name="raw_b")
         raw_a = sb.tile([P, PACK, Q], F32, name="raw_a")
-        words = [sb.tile([P, HALF], U32, name=f"words{h}", align_bytes=64) for h in range(2)]
+        pieces = [(0, HALF), (HALF, HALF)]
+        words = {first: sb.tile([P, width], U32, name=f"words{first}", align_bytes=64) for first, width in pieces}
         planes = sb.tile([P, T], U8, name="planes", align_bytes=64)
         lam_t = sb.tile([P, 1], F32, name="lam_t")
         damp_t = sb.tile([P, 1], F32, name="damp_t")
@@ -42,50 +43,60 @@ def tile_attend_turnedby_dampened_counts_heads_kernel(
 
         word_bytes = keys_words[0].rearrange("p n t -> p (n t)")
 
-        def load_words(h):
+        def load_words(first, width):
             nc.sync.dma_start(
-                out=words[h][:].bitcast(I32),
-                in_=word_bytes[:, PACK * HALF * h : PACK * HALF * (h + 1)].bitcast(I32),
+                out=words[first][:].bitcast(I32),
+                in_=word_bytes[:, PACK * first : PACK * (first + width)].bitcast(I32),
             )
 
-        nc.sync.dma_start(out=raw_b[:], in_=query2.rearrange("(p j) w -> p j w", j=PACK))
-        for quad in range(4):
-            nc.scalar.dma_start(
+        def load_scales(queue, quad):
+            queue.dma_start(
                 out=planes[32 * quad : 32 * quad + 4, :].bitcast(I32),
                 in_=keys_scales[0, 4 * quad : 4 * quad + 4, :].bitcast(I32),
             )
-        load_words(0)
+
+        for quad in range(2):
+            load_scales(nc.scalar, quad)
+        nc.sync.dma_start(out=raw_b[:], in_=query2.rearrange("(p j) w -> p j w", j=PACK))
+        for quad in range(2, 4):
+            load_scales(nc.sync, quad)
+        load_words(*pieces[0])
         nc.sync.dma_start(out=raw_a[:], in_=query.rearrange("(p j) w -> p j w", j=PACK))
-        load_words(1)
+        load_words(*pieces[1])
         nc.sync.dma_start(idx[:], offs)
         nc.sync.dma_start(idx2[:], offs2)
+        nc.sync.dma_start(out=lam_t[:], in_=lam)
+        nc.sync.dma_start(out=damp_t[:], in_=damp)
         nc.sync.dma_start(out=old_t[:], in_=old)
-        nc.gpsimd.dma_start(out=lam_t[:], in_=lam)
-        nc.gpsimd.dma_start(out=damp_t[:], in_=damp)
-        nc.gpsimd.dma_start(out=fade_t[:], in_=fade)
+        nc.sync.dma_start(out=fade_t[:], in_=fade)
 
         wf = sb.tile([P, T], F32, name="wf")
         nc.vector.memset(wf[:], 0.0)
 
-        def quantise(raw, name):
+        def quantise(raw, name, on_vector):
             grouped = sb.tile([P, Q, PACK], BF16, name=name + "_bf", align_bytes=64)
             codes = sb.tile([P, Q], U32, name=name + "_codes", align_bytes=64)
             scales = sb.tile([P, Q], U8, name=name + "_scales", align_bytes=64)
-            nc.vector.tensor_copy(out=grouped[:], in_=raw[:].rearrange("p j w -> p w j"))
+            by_column = raw[:].rearrange("p j w -> p w j")
+            if on_vector > 0:
+                nc.vector.tensor_copy(out=grouped[:, :on_vector, :], in_=by_column[:, :on_vector, :])
+            if on_vector < Q:
+                nc.scalar.activation(out=grouped[:, on_vector:, :], in_=by_column[:, on_vector:, :], func=ACT.Copy)
             nc.vector.quantize_mx(
                 out=codes[:].bitcast(FP8X4), scales=scales[:], in_=grouped[:].rearrange("p w j -> p (w j)")
             )
             return codes, scales
 
-        def score(operand, h, name):
+        def score(operand, first, width, name):
             codes, scales = operand
-            bank = ps.tile([P, HALF], F32, name=name)
+            held = max(start for start in words if start <= first)
+            bank = ps.tile([P, width], F32, name=name)
             nc.tensor.matmul_mx(
                 out=bank[:],
                 lhsT=codes[:].bitcast(FP8X4),
                 lhsT_scale=scales[:],
-                rhs=words[h][:].bitcast(FP8X4),
-                rhs_scale=planes[:, HALF * h : HALF * (h + 1)],
+                rhs=words[held][:, first - held : first - held + width].bitcast(FP8X4),
+                rhs_scale=planes[:, first : first + width],
                 start=True,
                 stop=True,
             )
@@ -94,40 +105,74 @@ def tile_attend_turnedby_dampened_counts_heads_kernel(
         a_sb = sb.tile([P, T], F32, name="a_sb")
         b_sb = sb.tile([P, T], F32, name="b_sb")
 
-        qb = quantise(raw_b, "qb")
-        b0 = score(qb, 0, "b0")
-        qa = quantise(raw_a, "qa")
-        nc.scalar.activation(out=b_sb[:, :HALF], in_=b0[:], func=ACT.Copy)
-        b1 = score(qb, 1, "b1")
-        nc.vector.tensor_copy(out=b_sb[:, HALF:], in_=b1[:])
-        a0 = score(qa, 0, "a0")
-        a1 = score(qa, 1, "a1")
-        nc.scalar.copy(out=a_sb[:, :HALF], in_=a0[:])
-        nc.scalar.copy(out=a_sb[:, HALF:], in_=a1[:])
+        qb = quantise(raw_b, "qb", 64)
+        qa = quantise(raw_a, "qa", 64)
+        b0 = score(qb, 0, HALF, "b0")
+        nc.scalar.copy(out=b_sb[:, :HALF], in_=b0[:])
+        for first in (HALF, HALF + HALF // 2):
+            bank = score(qb, first, HALF // 2, f"b{first}")
+            nc.vector.tensor_copy(out=b_sb[:, first : first + HALF // 2], in_=bank[:])
+        quarter = T // 4
+        a_banks = [score(qa, k * quarter, quarter, f"a{k}") for k in range(4)]
+
+        def empty_a(k):
+            cols = slice(k * quarter, (k + 1) * quarter)
+            if k % 2 == 0:
+                nc.scalar.copy(out=a_sb[:, cols], in_=a_banks[k][:])
+            else:
+                nc.vector.tensor_copy(out=a_sb[:, cols], in_=a_banks[k][:])
 
         b_at = sb.tile([P, I], F32, name="b_at")
         turn = sb.tile([P, I], F32, name="turn")
         a_at = sb.tile([P, I], F32, name="a_at")
-        a_at2 = sb.tile([P, I], F32, name="a_at2")
-        nc.vector.tensor_copy(out=b_at[:], in_=b_sb[:].indirect(idx[:]))
-        nc.scalar.activation(out=turn[:], in_=b_at[:], func=ACT.Tanh)
-        nc.vector.tensor_copy(out=a_at2[:], in_=a_sb[:].indirect(idx2[:]))
-        nc.scalar.activation(out=a_at[:], in_=a_sb[:].indirect(idx[:]), func=ACT.Copy)
-
         term = sb.tile([P, I], F32, name="term")
         s = sb.tile([P, I], F32, name="s")
         neg_max = sb.tile([P, 1], F32, name="neg_max")
-        nc.vector.scalar_tensor_tensor(
-            out=term[:], in0=turn[:], scalar=lam_t[:], in1=a_at2[:], op0=ALU.mult, op1=ALU.mult
-        )
-        nc.vector.tensor_tensor(out=s[:], in0=term[:], in1=a_at[:], op=ALU.add)
-        nc.vector.tensor_reduce(out=neg_max[:], in_=s[:], axis=mybir.AxisListType.X, op=ALU.max, negate=True)
+        halves = [(slice(k * I // 2, (k + 1) * I // 2), slice(k * I // 32, (k + 1) * I // 32)) for k in range(2)]
+        empty_a(0)
+        nc.vector.tensor_copy(out=b_at[:, halves[0][0]], in_=b_sb[:].indirect(idx[:, halves[0][1]]))
+        nc.scalar.activation(out=b_at[:, halves[1][0]], in_=b_sb[:].indirect(idx[:, halves[1][1]]), func=ACT.Copy)
+        for k in range(1, 4):
+            empty_a(k)
+        for slots, cols in halves:
+            nc.scalar.activation(out=turn[:, slots], in_=b_at[:, slots], func=ACT.Tanh)
+        for slots, cols in halves:
+            nc.scalar.activation(out=a_at[:, slots], in_=a_sb[:].indirect(idx[:, cols]), func=ACT.Copy)
+        for slots, cols in halves:
+            nc.vector.tensor_tensor(
+                out=term[:, slots], in0=a_sb[:].indirect(idx2[:, cols]), in1=turn[:, slots], op=ALU.mult
+            )
+        for slots, cols in halves:
+            nc.vector.scalar_tensor_tensor(
+                out=s[:, slots], in0=term[:, slots], scalar=lam_t[:], in1=a_at[:, slots], op0=ALU.mult, op1=ALU.add
+            )
+        neg_half = sb.tile([P, 2], F32, name="neg_half")
+        for k, (slots, cols) in enumerate(halves):
+            nc.vector.tensor_reduce(
+                out=neg_half[:, k : k + 1], in_=s[:, slots], axis=mybir.AxisListType.X, op=ALU.max, negate=True
+            )
+        nc.vector.tensor_tensor(out=neg_max[:], in0=neg_half[:, 0:1], in1=neg_half[:, 1:2], op=ALU.min)
 
+        e = sb.tile([P, I], F32, name="e")
+        e_sum = sb.tile([P, 2], F32, name="e_sum")
+        shift = sb.tile([P, 2], F32, name="shift")
+        shifted_sum = sb.tile([P, 2], F32, name="shifted_sum")
         p = sb.tile([P, I], F32, name="p")
         p_sum = sb.tile([P, 1], F32, name="p_sum")
         p_inv = sb.tile([P, 1], F32, name="p_inv")
         gain = sb.tile([P, 1], F32, name="gain")
-        nc.scalar.activation(out=p[:], in_=s[:], func=ACT.Exp, bias=neg_max[:], accum_out=p_sum[:])
+        for k, (slots, cols) in enumerate(halves):
+            nc.scalar.activation(
+                out=e[:, slots], in_=s[:, slots], func=ACT.Exp, bias=neg_half[:, k : k + 1], accum_out=e_sum[:, k : k + 1]
+            )
+        nc.scalar.activation(out=shift[:], in_=neg_half[:], func=ACT.Exp, scale=-1.0, bias=neg_max[:])
+        nc.vector.scalar_tensor_tensor(
+            out=shifted_sum[:], in0=e_sum[:], scalar=1.0, in1=shift[:], op0=ALU.mult, op1=ALU.mult, accum_out=p_sum[:]
+        )
+        for k, (slots, cols) in enumerate(halves):
+            nc.vector.tensor_scalar(
+                out=p[:, slots], in0=e[:, slots], scalar1=shift[:, k : k + 1], scalar2=None, op0=ALU.mult
+            )
         nc.vector.reciprocal(out=p_inv[:], in_=p_sum[:])
         nc.vector.tensor_scalar(
             out=gain[:], in0=p_inv[:], scalar1=damp_t[:], scalar2=float(I), op0=ALU.mult, op1=ALU.mult

from contextlib import ExitStack

import concourse.mybir as mybir

D, T, I, Q = 512, 1024, 512, 128
FLOPS = 2 * 2 * D * T * Q

F32 = mybir.dt.float32
BF16 = mybir.dt.bfloat16
I32 = mybir.dt.int32
U32 = mybir.dt.uint32
U16 = mybir.dt.uint16
U8 = mybir.dt.uint8
FP8X4 = mybir.dt.float8_e4m3fn_x4
ALU = mybir.AluOpType
ACT = mybir.ActivationFunctionType

P = 128
PACK = 4
HALF = T // 2
STORE = 256


def tile_attend_turnedby_dampened_counts_heads_kernel(
    tc, query, query2, keys_words, keys_scales, lam, damp, old, fade, offs, offs2, out
):
    nc = tc.nc
    with ExitStack() as ctx:
        sb = ctx.enter_context(tc.tile_pool(name="sb", bufs=1))
        ps = ctx.enter_context(tc.psum_pool(name="ps", bufs=1))

        idx = sb.tile([P, I // 16], U16, name="idx")
        idx2 = sb.tile([P, I // 16], U16, name="idx2")
        raw_b = sb.tile([P, PACK, Q], F32, name="raw_b")
        raw_a = sb.tile([P, PACK, Q], F32, name="raw_a")
        pieces = [(0, HALF), (HALF, HALF)]
        words = {first: sb.tile([P, width], U32, name=f"words{first}", align_bytes=64) for first, width in pieces}
        planes = sb.tile([P, T], U8, name="planes", align_bytes=64)
        lam_t = sb.tile([P, 1], F32, name="lam_t")
        damp_t = sb.tile([P, 1], F32, name="damp_t")
        fade_t = sb.tile([P, 1], F32, name="fade_t")
        old_t = sb.tile([P, T], F32, name="old_t")

        word_bytes = keys_words[0].rearrange("p n t -> p (n t)")

        def load_words(first, width):
            nc.sync.dma_start(
                out=words[first][:].bitcast(I32),
                in_=word_bytes[:, PACK * first : PACK * (first + width)].bitcast(I32),
            )

        def load_scales(queue, quad):
            queue.dma_start(
                out=planes[32 * quad : 32 * quad + 4, :].bitcast(I32),
                in_=keys_scales[0, 4 * quad : 4 * quad + 4, :].bitcast(I32),
            )

        for quad in range(2):
            load_scales(nc.scalar, quad)
        nc.sync.dma_start(out=raw_b[:], in_=query2.rearrange("(p j) w -> p j w", j=PACK))
        for quad in range(2, 4):
            load_scales(nc.sync, quad)
        load_words(*pieces[0])
        nc.sync.dma_start(out=raw_a[:], in_=query.rearrange("(p j) w -> p j w", j=PACK))
        load_words(*pieces[1])
        nc.sync.dma_start(idx[:], offs)
        nc.sync.dma_start(idx2[:], offs2)
        nc.sync.dma_start(out=lam_t[:], in_=lam)
        nc.sync.dma_start(out=damp_t[:], in_=damp)
        nc.sync.dma_start(out=old_t[:], in_=old)
        nc.sync.dma_start(out=fade_t[:], in_=fade)

        wf = sb.tile([P, T], F32, name="wf")
        nc.vector.memset(wf[:], 0.0)

        def quantise(raw, name, on_vector):
            grouped = sb.tile([P, Q, PACK], BF16, name=name + "_bf", align_bytes=64)
            codes = sb.tile([P, Q], U32, name=name + "_codes", align_bytes=64)
            scales = sb.tile([P, Q], U8, name=name + "_scales", align_bytes=64)
            by_column = raw[:].rearrange("p j w -> p w j")
            if on_vector > 0:
                nc.vector.tensor_copy(out=grouped[:, :on_vector, :], in_=by_column[:, :on_vector, :])
            if on_vector < Q:
                nc.scalar.activation(out=grouped[:, on_vector:, :], in_=by_column[:, on_vector:, :], func=ACT.Copy)
            nc.vector.quantize_mx(
                out=codes[:].bitcast(FP8X4), scales=scales[:], in_=grouped[:].rearrange("p w j -> p (w j)")
            )
            return codes, scales

        def score(operand, first, width, name):
            codes, scales = operand
            held = max(start for start in words if start <= first)
            bank = ps.tile([P, width], F32, name=name)
            nc.tensor.matmul_mx(
                out=bank[:],
                lhsT=codes[:].bitcast(FP8X4),
                lhsT_scale=scales[:],
                rhs=words[held][:, first - held : first - held + width].bitcast(FP8X4),
                rhs_scale=planes[:, first : first + width],
                start=True,
                stop=True,
            )
            return bank

        a_sb = sb.tile([P, T], F32, name="a_sb")
        b_sb = sb.tile([P, T], F32, name="b_sb")

        qb = quantise(raw_b, "qb", 64)
        qa = quantise(raw_a, "qa", 64)
        b0 = score(qb, 0, HALF, "b0")
        nc.scalar.copy(out=b_sb[:, :HALF], in_=b0[:])
        for first in (HALF, HALF + HALF // 2):
            bank = score(qb, first, HALF // 2, f"b{first}")
            nc.vector.tensor_copy(out=b_sb[:, first : first + HALF // 2], in_=bank[:])
        quarter = T // 4
        a_banks = [score(qa, k * quarter, quarter, f"a{k}") for k in range(4)]

        def empty_a(k):
            cols = slice(k * quarter, (k + 1) * quarter)
            if k % 2 == 0:
                nc.scalar.copy(out=a_sb[:, cols], in_=a_banks[k][:])
            else:
                nc.vector.tensor_copy(out=a_sb[:, cols], in_=a_banks[k][:])

        b_at = sb.tile([P, I], F32, name="b_at")
        turn = sb.tile([P, I], F32, name="turn")
        a_at = sb.tile([P, I], F32, name="a_at")
        term = sb.tile([P, I], F32, name="term")
        s = sb.tile([P, I], F32, name="s")
        neg_max = sb.tile([P, 1], F32, name="neg_max")
        halves = [(slice(k * I // 2, (k + 1) * I // 2), slice(k * I // 32, (k + 1) * I // 32)) for k in range(2)]
        empty_a(0)
        nc.vector.tensor_copy(out=b_at[:, halves[0][0]], in_=b_sb[:].indirect(idx[:, halves[0][1]]))
        nc.scalar.activation(out=b_at[:, halves[1][0]], in_=b_sb[:].indirect(idx[:, halves[1][1]]), func=ACT.Copy)
        for k in range(1, 4):
            empty_a(k)
        for slots, cols in halves:
            nc.scalar.activation(out=turn[:, slots], in_=b_at[:, slots], func=ACT.Tanh)
        for slots, cols in halves:
            nc.scalar.activation(out=a_at[:, slots], in_=a_sb[:].indirect(idx[:, cols]), func=ACT.Copy)
        for slots, cols in halves:
            nc.vector.tensor_tensor(
                out=term[:, slots], in0=a_sb[:].indirect(idx2[:, cols]), in1=turn[:, slots], op=ALU.mult
            )
        for slots, cols in halves:
            nc.vector.scalar_tensor_tensor(
                out=s[:, slots], in0=term[:, slots], scalar=lam_t[:], in1=a_at[:, slots], op0=ALU.mult, op1=ALU.add
            )
        neg_half = sb.tile([P, 2], F32, name="neg_half")
        for k, (slots, cols) in enumerate(halves):
            nc.vector.tensor_reduce(
                out=neg_half[:, k : k + 1], in_=s[:, slots], axis=mybir.AxisListType.X, op=ALU.max, negate=True
            )
        nc.vector.tensor_tensor(out=neg_max[:], in0=neg_half[:, 0:1], in1=neg_half[:, 1:2], op=ALU.min)

        e = sb.tile([P, I], F32, name="e")
        e_sum = sb.tile([P, 2], F32, name="e_sum")
        shift = sb.tile([P, 2], F32, name="shift")
        shifted_sum = sb.tile([P, 2], F32, name="shifted_sum")
        p = sb.tile([P, I], F32, name="p")
        p_sum = sb.tile([P, 1], F32, name="p_sum")
        p_inv = sb.tile([P, 1], F32, name="p_inv")
        gain = sb.tile([P, 1], F32, name="gain")
        for k, (slots, cols) in enumerate(halves):
            nc.scalar.activation(
                out=e[:, slots], in_=s[:, slots], func=ACT.Exp, bias=neg_half[:, k : k + 1], accum_out=e_sum[:, k : k + 1]
            )
        nc.scalar.activation(out=shift[:], in_=neg_half[:], func=ACT.Exp, scale=-1.0, bias=neg_max[:])
        nc.vector.scalar_tensor_tensor(
            out=shifted_sum[:], in0=e_sum[:], scalar=1.0, in1=shift[:], op0=ALU.mult, op1=ALU.mult, accum_out=p_sum[:]
        )
        for k, (slots, cols) in enumerate(halves):
            nc.vector.tensor_scalar(
                out=p[:, slots], in0=e[:, slots], scalar1=shift[:, k : k + 1], scalar2=None, op0=ALU.mult
            )
        nc.vector.reciprocal(out=p_inv[:], in_=p_sum[:])
        nc.vector.tensor_scalar(
            out=gain[:], in0=p_inv[:], scalar1=damp_t[:], scalar2=float(I), op0=ALU.mult, op1=ALU.mult
        )

        part = sb.tile([P, I], F32, name="part")
        part_sum = sb.tile([P, 1], F32, name="part_sum")
        part_inv = sb.tile([P, 1], F32, name="part_inv")
        ws = sb.tile([P, I], F32, name="ws")
        nc.scalar.activation(out=part[:], in_=p[:], func=ACT.Ln, scale=gain[:], bias=1.0, accum_out=part_sum[:])
        nc.vector.reciprocal(out=part_inv[:], in_=part_sum[:])
        nc.vector.tensor_scalar(
            out=ws[:], in0=part[:], scalar1=part_inv[:], scalar2=float(I), op0=ALU.mult, op1=ALU.mult
        )
        nc.vector.tensor_copy(out=wf[:].indirect(idx[:]), in_=ws[:])

        for c in range(T // STORE):
            cols = slice(STORE * c, STORE * (c + 1))
            y = sb.tile([P, STORE], F32, name=f"y{c}")
            nc.vector.scalar_tensor_tensor(
                out=y[:], in0=old_t[:, cols], scalar=fade_t[:], in1=wf[:, cols], op0=ALU.mult, op1=ALU.add
            )
            queue = nc.sync if c % 2 == 0 else nc.scalar
            queue.dma_start(out=out[:, cols], in_=y[:])
